import numpy as np
import ml_dtypes


def mxq(x, axis, fmt="e4m3"):
    dtype, down = {"e4m3": (ml_dtypes.float8_e4m3fn, 7), "e5m2": (ml_dtypes.float8_e5m2, 14)}[fmt]
    v = np.moveaxis(np.asarray(x, np.float32).astype(ml_dtypes.bfloat16).astype(np.float64), axis, -1)
    blocks = v.reshape(v.shape[:-1] + (-1, 32))
    amax = np.abs(blocks).max(-1, keepdims=True)
    byte = np.maximum(np.where(amax > 0, np.frexp(amax)[1] - 1 + 127, 0) - down, 1)
    scale = np.exp2(byte - 127.0)
    codes = (blocks / scale).astype(np.float32).astype(dtype).astype(np.float64)
    return np.moveaxis((codes * scale).reshape(v.shape), -1, axis)


WIDE = False


def mx_kscale(k):
    if not WIDE:
        return np.ones(k)
    levels = np.array([10, -10, 5, -5, 0])
    if k % 512:
        return np.exp2(np.random.permutation(np.resize(levels, k // 32))).repeat(32)
    a = np.empty((k // 512, 16))
    for p in range(k // 512):
        a[p, :8] = np.random.permutation(np.resize(levels, 8))
        for g in range(8):
            far = levels[np.abs(levels - a[p, g]) >= 10]
            a[p, g + 8] = far[np.random.randint(len(far))]
    return np.exp2(a.ravel()).repeat(32)


def f64(x):
    return np.asarray(x).astype(np.float64)


def striped(idx):
    return np.tile(idx.reshape(-1, 16).T, (8, 1)).astype(np.uint16)


def unstriped(offs):
    return offs[:16].T.reshape(-1).astype(np.int64)


def pack_weight(w):
    k, n = w.shape
    w = f64(np.asarray(w, np.float32).astype(ml_dtypes.bfloat16)).reshape(k // 32, 32, n)
    amax = np.abs(w).max(1)
    byte = np.clip(np.where(amax > 0, np.frexp(amax)[1] - 1 + 127 - 7, 1), 1, 254)
    scaled = (w * np.exp2(127.0 - byte)[:, None, :]).reshape(k, n).astype(np.float32)
    words = np.ascontiguousarray(scaled.reshape(k // 512, 128, 4, n).transpose(0, 1, 3, 2)).astype(ml_dtypes.float8_e4m3fn).view(np.uint8)
    return words, np.ascontiguousarray(byte.astype(np.uint8).reshape(k // 512, 16, n))


def unpack_weight(words, scales):
    g, p, n, _ = words.shape
    vals = np.ascontiguousarray(words).view(ml_dtypes.float8_e4m3fn).astype(np.float64) * np.repeat(np.exp2(scales.astype(np.float64) - 127.0), 8, axis=1)[..., None]
    return vals.transpose(0, 1, 3, 2).reshape(g * 512, n)


def sigmoid(v):
    return 1.0 / (1.0 + np.exp(-np.maximum(v, -700.0)))

def planes(y):
    n, m = y.shape
    v = y.astype(np.float32).astype(ml_dtypes.bfloat16).astype(np.float64).reshape(n // 32, 32, m)
    top = np.abs(v).max(1)
    byte = np.clip(np.where(top > 0, np.frexp(top)[1] - 1 + 127 - 7, 1), 1, 254)
    codes = (v * np.exp2(127.0 - byte)[:, None, :]).reshape(n, m).astype(np.float32).astype(ml_dtypes.float8_e4m3fn).view(np.uint8)
    words = codes.reshape(n // 512, 128, 4, m).transpose(0, 1, 3, 2)
    return np.ascontiguousarray(words), np.ascontiguousarray(byte.astype(np.uint8).reshape(n // 512, 16, m))


K, T, S, N = 512, 1024, 512, 512


def setup_inputs():
    n = np.random.standard_normal
    s = mx_kscale(K)[:, None]
    packed_xT = pack_weight(n((K, T)) * s)
    return {
        "x_words": packed_xT[0],
        "x_scales": packed_xT[1],
        "side": n((N, T)).astype(np.float32),
        "w1": (n((K, N)) / np.sqrt(K) / s).astype(np.float32),
        "offs": striped(np.random.permutation(T)[:S]),
    }


def reference(x_words, x_scales, side, w1, offs):
    xq = unpack_weight(x_words, x_scales)[:, unstriped(offs)]
    y = mxq(f64(w1), 0, "e4m3").T @ xq
    g = f64(side)[:, unstriped(offs)]
    out_0 = y * sigmoid(g)
    return (out_0,) + planes(out_0)

@@ -1,0 +1,99 @@
+import concourse.mybir as mybir
+
+K, T, S, N = 512, 1024, 512, 512
+FLOPS = 2 * K * S * N
+
+F32 = mybir.dt.float32
+BF16 = mybir.dt.bfloat16
+I32 = mybir.dt.int32
+U32 = mybir.dt.uint32
+U16 = mybir.dt.uint16
+U8 = mybir.dt.uint8
+FP8X4 = mybir.dt.float8_e4m3fn_x4
+SIGMOID = mybir.ActivationFunctionType.Sigmoid
+MULT = mybir.AluOpType.mult
+
+P = 128
+PACK = 4
+HALF = S // 2
+
+
+def tile_picked_sidegate_sigmoid_po_kernel(tc, x_words, x_scales, side, w1, offs, out_0, out_1, out_2):
+    nc = tc.nc
+    with tc.tile_pool(name="keep", bufs=1) as keep, tc.psum_pool(name="psum", bufs=1) as psum:
+        offsets = keep.tile([P, S // 16], U16, name="offsets")
+        words_all = keep.tile([P, T], I32, name="words_all")
+        scales_all = keep.tile([P, T], U8, name="scales_all")
+        w_raw = [keep.tile([P, PACK, N // 2], F32, name=f"w_raw{h}") for h in range(2)]
+        side_all = [keep.tile([P, T], F32, name=f"side_all{t}") for t in range(PACK)]
+        warm = keep.tile([P, 8], F32, name="warm")
+        warm_out = keep.tile([P, 8], F32, name="warm_out")
+
+        nc.vector.memset(scales_all[:].bitcast(I32), 0)
+        nc.gpsimd.memset(warm[:], 0.0)
+        nc.scalar.activation(warm_out[:], warm[:], SIGMOID)
+
+        w_rows = w1.rearrange("(p j) c -> p j c", j=PACK)
+        side_rows = side.rearrange("(p t) c -> p t c", t=PACK)
+        nc.sync.dma_start(offsets[:], offs)
+        nc.sync.dma_start(words_all[:], x_words[0].rearrange("p c r -> p (c r)").bitcast(I32))
+        for q in range(4):
+            nc.sync.dma_start(scales_all[32 * q : 32 * q + 4, :].bitcast(I32), x_scales[0, 4 * q : 4 * q + 4, :].bitcast(I32))
+        for h in range(2):
+            nc.sync.dma_start(w_raw[h][:], w_rows[:, :, h * (N // 2) : (h + 1) * (N // 2)])
+        for t in range(PACK):
+            nc.sync.dma_start(side_all[t][:], side_rows[:, t, :])
+
+        x_codes = keep.tile([P, S], U32, name="x_codes", align_bytes=64)
+        x_bytes = keep.tile([P, S], U8, name="x_bytes", align_bytes=64)
+        nc.vector.tensor_copy(x_codes[:], words_all[:].bitcast(U32).indirect(offsets[:]))
+        nc.vector.tensor_copy(x_bytes[:], scales_all[:].indirect(offsets[:]))
+
+        w_bf = [keep.tile([P, PACK, P // 2, PACK], BF16, name=f"w_bf{h}", align_bytes=64) for h in range(2)]
+        nc.scalar.copy(w_bf[0][:].rearrange("p t m j -> p m j t"), w_raw[0][:].rearrange("p j (m t) -> p m j t", t=PACK))
+        nc.vector.tensor_copy(w_bf[1][:].rearrange("p t m j -> p m j t"), w_raw[1][:].rearrange("p j (m t) -> p m j t", t=PACK))
+
+        w_codes = [keep.tile([P, P], U32, name=f"w_codes{t}", align_bytes=64) for t in range(PACK)]
+        w_bytes = [keep.tile([P, P], U8, name=f"w_bytes{t}", align_bytes=64) for t in range(PACK)]
+        for h in range(2):
+            cols = slice(h * (P // 2), (h + 1) * (P // 2))
+            for t in range(PACK):
+                nc.vector.quantize_mx(out=w_codes[t][:, cols].bitcast(FP8X4), scales=w_bytes[t][:, cols],
+                                      in_=w_bf[h][:, t, :, :].rearrange("p m j -> p (m j)"))
+
+        acc = [psum.tile([P, S], F32, name=f"acc{t}") for t in range(PACK)]
+        for t in range(PACK):
+            nc.tensor.matmul_mx(out=acc[t][:], lhsT=w_codes[t][:].bitcast(FP8X4), lhsT_scale=w_bytes[t][:],
+                                rhs=x_codes[:].bitcast(FP8X4), rhs_scale=x_bytes[:], start=True, stop=True)
+
+        y = keep.tile([P, PACK, S], F32, name="y")
+        out_rows = out_0.rearrange("(p t) s -> p t s", t=PACK)
+        for t in range(PACK - 1):
+            gate = keep.tile([P, S], F32, name=f"gate{t}")
+            nc.scalar.activation(gate[:], side_all[t][:].indirect(offsets[:]), SIGMOID)
+            nc.vector.tensor_tensor(y[:, t, :], acc[t][:], gate[:], MULT)
+            nc.sync.dma_start(out_rows[:, t, :], y[:, t, :])
+
+        y_codes = keep.tile([P, S], U32, name="y_codes", align_bytes=64)
+        y_bytes = keep.tile([P, S], U8, name="y_bytes", align_bytes=64)
+        t = PACK - 1
+        y_bf = []
+        for h in range(2):
+            cols = slice(h * HALF, (h + 1) * HALF)
+            gate = keep.tile([P, HALF], F32, name=f"gate_last{h}")
+            nc.scalar.activation(gate[:], side_all[t][:].indirect(offsets[:, h * HALF // 16 : (h + 1) * HALF // 16]), SIGMOID)
+            nc.vector.tensor_tensor(y[:, t, cols], acc[t][:, cols], gate[:], MULT)
+            grouped = keep.tile([P, HALF, PACK], BF16, name=f"y_bf{h}", align_bytes=64)
+            nc.vector.tensor_copy(grouped[:].rearrange("p (c i) t -> p c t i", i=4),
+                                  y[:, :, cols].rearrange("p t (c i) -> p c t i", i=4))
+            y_bf.append(grouped)
+        nc.sync.dma_start(out_rows[:, t, :], y[:, t, :])
+        words_out = out_1[0].rearrange("p c r -> p (c r)").bitcast(I32)
+        for h in range(2):
+            cols = slice(h * HALF, (h + 1) * HALF)
+            nc.vector.quantize_mx(out=y_codes[:, cols].bitcast(FP8X4), scales=y_bytes[:, cols],
+                                  in_=y_bf[h][:].rearrange("p c t -> p (c t)"))
+            nc.sync.dma_start(words_out[:, cols], y_codes[:, cols].bitcast(I32))
+        for q in range(4):
+            queue = nc.sync if q % 2 == 0 else nc.scalar
+            queue.dma_start(out_2[0, 4 * q : 4 * q + 4, :].bitcast(I32), y_bytes[32 * q : 32 * q + 4, :].bitcast(I32))

@@ -16,6 +16,8 @@ MULT = mybir.AluOpType.mult
 P = 128
 PACK = 4
 HALF = S // 2
+M_VECTOR = 88
+PRE = True
 
 
 def tile_picked_sidegate_sigmoid_po_kernel(tc, x_words, x_scales, side, w1, offs, out_0, out_1, out_2):
@@ -24,76 +26,110 @@ def tile_picked_sidegate_sigmoid_po_kernel(tc, x_words, x_scales, side, w1, offs
         offsets = keep.tile([P, S // 16], U16, name="offsets")
         words_all = keep.tile([P, T], I32, name="words_all")
         scales_all = keep.tile([P, T], U8, name="scales_all")
-        w_raw = [keep.tile([P, PACK, N // 2], F32, name=f"w_raw{h}") for h in range(2)]
+        w_raw = keep.tile([P, PACK, N], F32, name="w_raw")
         side_all = [keep.tile([P, T], F32, name=f"side_all{t}") for t in range(PACK)]
         warm = keep.tile([P, 8], F32, name="warm")
         warm_out = keep.tile([P, 8], F32, name="warm_out")
 
-        nc.vector.memset(scales_all[:].bitcast(I32), 0)
+        nc.gpsimd.memset(scales_all[:].bitcast(I32), 0)
         nc.gpsimd.memset(warm[:], 0.0)
         nc.scalar.activation(warm_out[:], warm[:], SIGMOID)
 
-        w_rows = w1.rearrange("(p j) c -> p j c", j=PACK)
         side_rows = side.rearrange("(p t) c -> p t c", t=PACK)
-        nc.sync.dma_start(offsets[:], offs)
-        nc.sync.dma_start(words_all[:], x_words[0].rearrange("p c r -> p (c r)").bitcast(I32))
-        for q in range(4):
-            nc.sync.dma_start(scales_all[32 * q : 32 * q + 4, :].bitcast(I32), x_scales[0, 4 * q : 4 * q + 4, :].bitcast(I32))
-        for h in range(2):
-            nc.sync.dma_start(w_raw[h][:], w_rows[:, :, h * (N // 2) : (h + 1) * (N // 2)])
-        for t in range(PACK):
-            nc.sync.dma_start(side_all[t][:], side_rows[:, t, :])
+
+        def load(what):
+            if what == "x":
+                nc.sync.dma_start(words_all[:], x_words[0].rearrange("p c r -> p (c r)").bitcast(I32))
+            elif what == "o":
+                nc.sync.dma_start(offsets[:], offs)
+            elif what == "b":
+                for q in range(4):
+                    nc.sync.dma_start(scales_all[32 * q : 32 * q + 4, :].bitcast(I32), x_scales[0, 4 * q : 4 * q + 4, :].bitcast(I32))
+            elif what == "w":
+                nc.sync.dma_start(w_raw[:], w1.rearrange("(p j) c -> p j c", j=PACK))
+            else:
+                t = int(what[1])
+                nc.sync.dma_start(side_all[t][:], side_rows[:, t, :])
+
+        for what in ["x","o","b","w","s0","s1","s2","s3"]:
+            load(what)
 
         x_codes = keep.tile([P, S], U32, name="x_codes", align_bytes=64)
-        x_bytes = keep.tile([P, S], U8, name="x_bytes", align_bytes=64)
         nc.vector.tensor_copy(x_codes[:], words_all[:].bitcast(U32).indirect(offsets[:]))
+        x_bytes = keep.tile([P, S], U8, name="x_bytes", align_bytes=64)
         nc.vector.tensor_copy(x_bytes[:], scales_all[:].indirect(offsets[:]))
 
-        w_bf = [keep.tile([P, PACK, P // 2, PACK], BF16, name=f"w_bf{h}", align_bytes=64) for h in range(2)]
-        nc.scalar.copy(w_bf[0][:].rearrange("p t m j -> p m j t"), w_raw[0][:].rearrange("p j (m t) -> p m j t", t=PACK))
-        nc.vector.tensor_copy(w_bf[1][:].rearrange("p t m j -> p m j t"), w_raw[1][:].rearrange("p j (m t) -> p m j t", t=PACK))
-
-        w_codes = [keep.tile([P, P], U32, name=f"w_codes{t}", align_bytes=64) for t in range(PACK)]
-        w_bytes = [keep.tile([P, P], U8, name=f"w_bytes{t}", align_bytes=64) for t in range(PACK)]
-        for h in range(2):
-            cols = slice(h * (P // 2), (h + 1) * (P // 2))
-            for t in range(PACK):
-                nc.vector.quantize_mx(out=w_codes[t][:, cols].bitcast(FP8X4), scales=w_bytes[t][:, cols],
-                                      in_=w_bf[h][:, t, :, :].rearrange("p m j -> p (m j)"))
+        w_bf = keep.tile([P, PACK, P, PACK], BF16, name="w_bf", align_bytes=64)
+        w_dst = w_bf[:].rearrange("p t m j -> p m j t")
+        w_src = w_raw[:].rearrange("p j (m t) -> p m j t", t=PACK)
+        nc.vector.tensor_copy(w_dst[:, :M_VECTOR], w_src[:, :M_VECTOR])
+        nc.scalar.copy(w_dst[:, M_VECTOR:], w_src[:, M_VECTOR:])
 
         acc = [psum.tile([P, S], F32, name=f"acc{t}") for t in range(PACK)]
-        for t in range(PACK):
-            nc.tensor.matmul_mx(out=acc[t][:], lhsT=w_codes[t][:].bitcast(FP8X4), lhsT_scale=w_bytes[t][:],
-                                rhs=x_codes[:].bitcast(FP8X4), rhs_scale=x_bytes[:], start=True, stop=True)
+        for t0, t1 in [(0,1),(1,2),(2,4)]:
+            w_codes = keep.tile([P, (t1 - t0) * P], U32, name=f"w_codes{t0}", align_bytes=64)
+            w_bytes = keep.tile([P, (t1 - t0) * P], U8, name=f"w_bytes{t0}", align_bytes=64)
+            nc.vector.quantize_mx(out=w_codes[:].bitcast(FP8X4), scales=w_bytes[:],
+                                  in_=w_bf[:, t0:t1, :, :].rearrange("p t m j -> p (t m j)"))
+            for t in range(t0, t1):
+                cols = slice((t - t0) * P, (t - t0 + 1) * P)
+                nc.tensor.matmul_mx(out=acc[t][:], lhsT=w_codes[:, cols].bitcast(FP8X4), lhsT_scale=w_bytes[:, cols],
+                                    rhs=x_codes[:].bitcast(FP8X4), rhs_scale=x_bytes[:], start=True, stop=True)
 
         y = keep.tile([P, PACK, S], F32, name="y")
         out_rows = out_0.rearrange("(p t) s -> p t s", t=PACK)
-        for t in range(PACK - 1):
-            gate = keep.tile([P, S], F32, name=f"gate{t}")
-            nc.scalar.activation(gate[:], side_all[t][:].indirect(offsets[:]), SIGMOID)
-            nc.vector.tensor_tensor(y[:, t, :], acc[t][:], gate[:], MULT)
-            nc.sync.dma_start(out_rows[:, t, :], y[:, t, :])
+        units = [(0,256),(256,384),(384,512)]
+        grouped = {u: keep.tile([P, u[1] - u[0], PACK], BF16, name=f"grouped{u[0]}", align_bytes=64) for u in units}
+
+        def part(a, b):
+            u = [u for u in units if u[0] <= a and b <= u[1]][0]
+            return grouped[u][:, a - u[0] : b - u[0], :]
 
         y_codes = keep.tile([P, S], U32, name="y_codes", align_bytes=64)
         y_bytes = keep.tile([P, S], U8, name="y_bytes", align_bytes=64)
-        t = PACK - 1
-        y_bf = []
-        for h in range(2):
-            cols = slice(h * HALF, (h + 1) * HALF)
-            gate = keep.tile([P, HALF], F32, name=f"gate_last{h}")
-            nc.scalar.activation(gate[:], side_all[t][:].indirect(offsets[:, h * HALF // 16 : (h + 1) * HALF // 16]), SIGMOID)
-            nc.vector.tensor_tensor(y[:, t, cols], acc[t][:, cols], gate[:], MULT)
-            grouped = keep.tile([P, HALF, PACK], BF16, name=f"y_bf{h}", align_bytes=64)
-            nc.vector.tensor_copy(grouped[:].rearrange("p (c i) t -> p c t i", i=4),
-                                  y[:, :, cols].rearrange("p t (c i) -> p c t i", i=4))
-            y_bf.append(grouped)
-        nc.sync.dma_start(out_rows[:, t, :], y[:, t, :])
         words_out = out_1[0].rearrange("p c r -> p (c r)").bitcast(I32)
-        for h in range(2):
-            cols = slice(h * HALF, (h + 1) * HALF)
-            nc.vector.quantize_mx(out=y_codes[:, cols].bitcast(FP8X4), scales=y_bytes[:, cols],
-                                  in_=y_bf[h][:].rearrange("p c t -> p (c t)"))
-            nc.sync.dma_start(words_out[:, cols], y_codes[:, cols].bitcast(I32))
+
+        def gated(t, a, b):
+            gate = keep.tile([P, b - a], F32, name=f"gate{t}_{a}")
+            nc.scalar.activation(gate[:], side_all[t][:].indirect(offsets[:, a // 16 : b // 16]), SIGMOID)
+            nc.vector.tensor_tensor(y[:, t, a:b], acc[t][:, a:b], gate[:], MULT)
+
+        def gated_by_vector(t, a, b):
+            picked = keep.tile([P, b - a], F32, name=f"picked{t}_{a}")
+            gate = keep.tile([P, b - a], F32, name=f"gate{t}_{a}")
+            nc.vector.tensor_copy(picked[:], side_all[t][:].indirect(offsets[:, a // 16 : b // 16]))
+            nc.scalar.activation(gate[:], picked[:], SIGMOID)
+            nc.vector.tensor_tensor(y[:, t, a:b], acc[t][:, a:b], gate[:], MULT)
+
+        def weave(a, b, t0, t1, scalar):
+            if t1 - t0 == PACK:
+                dst = part(a, b).rearrange("p (c i) t -> p c t i", i=4)
+                src = y[:, :, a:b].rearrange("p t (c i) -> p c t i", i=4)
+            else:
+                dst = part(a, b)[:, :, t0:t1]
+                src = y[:, t0:t1, a:b].rearrange("p t c -> p c t")
+            if scalar:
+                nc.scalar.copy(dst, src)
+            else:
+                nc.vector.tensor_copy(dst, src)
+
+        def quantise(a, b):
+            nc.vector.quantize_mx(out=y_codes[:, a:b].bitcast(FP8X4), scales=y_bytes[:, a:b],
+                                  in_=part(a, b).rearrange("p c t -> p (c t)"))
+
+        for step in [["g",0,0,256],["g",0,256,512],["g",1,0,256],["w",0,256,0,2,False],["g",1,256,512],["y",0,2],["w",256,384,0,2,False],["w",384,512,0,2,False],["g",2,0,256],["g",2,256,512],["y",2,3],["g",3,0,128],["g",3,128,256],["w",0,256,2,4,False],["g",3,256,384],["q",0,256],["c",0,256],["g",3,384,512],["y",3,4],["w",256,384,2,4,True],["w",384,512,2,4,False],["q",384,512],["q",256,384],["c",256,512]]:
+            if step[0] == "g":
+                gated(step[1], step[2], step[3])
+            elif step[0] == "v":
+                gated_by_vector(step[1], step[2], step[3])
+            elif step[0] == "w":
+                weave(step[1], step[2], step[3], step[4], step[5])
+            elif step[0] == "q":
+                quantise(step[1], step[2])
+            elif step[0] == "y":
+                nc.sync.dma_start(out_rows[:, step[1] : step[2], :], y[:, step[1] : step[2], :])
+            elif step[0] == "c":
+                nc.sync.dma_start(words_out[:, step[1] : step[2]], y_codes[:, step[1] : step[2]].bitcast(I32))
         for q in range(4):
-            queue = nc.sync if q % 2 == 0 else nc.scalar
+            queue = nc.scalar if q % 2 == 0 else nc.sync
             queue.dma_start(out_2[0, 4 * q : 4 * q + 4, :].bitcast(I32), y_bytes[32 * q : 32 * q + 4, :].bitcast(I32))

@@ -16,7 +16,7 @@ MULT = mybir.AluOpType.mult
 P = 128
 PACK = 4
 HALF = S // 2
-M_VECTOR = 88
+M_VECTOR = 80
 PRE = True
 
 
@@ -31,7 +31,7 @@ def tile_picked_sidegate_sigmoid_po_kernel(tc, x_words, x_scales, side, w1, offs
         warm = keep.tile([P, 8], F32, name="warm")
         warm_out = keep.tile([P, 8], F32, name="warm_out")
 
-        nc.gpsimd.memset(scales_all[:].bitcast(I32), 0)
+        nc.vector.memset(scales_all[:].bitcast(I32), 0)
         nc.gpsimd.memset(warm[:], 0.0)
         nc.scalar.activation(warm_out[:], warm[:], SIGMOID)
 
@@ -65,7 +65,13 @@ def tile_picked_sidegate_sigmoid_po_kernel(tc, x_words, x_scales, side, w1, offs
         nc.vector.tensor_copy(w_dst[:, :M_VECTOR], w_src[:, :M_VECTOR])
         nc.scalar.copy(w_dst[:, M_VECTOR:], w_src[:, M_VECTOR:])
 
-        acc = [psum.tile([P, S], F32, name=f"acc{t}") for t in range(PACK)]
+        spans = {t: [(0, HALF), (HALF, S)] if t == 0 else [(0, S)] for t in range(PACK)}
+        banks = {(t, u): psum.tile([P, u[1] - u[0]], F32, name=f"acc{t}_{u[0]}") for t in range(PACK) for u in spans[t]}
+
+        def product(t, a, b):
+            u = [u for u in spans[t] if u[0] <= a and b <= u[1]][0]
+            return banks[t, u][:, a - u[0] : b - u[0]]
+
         for t0, t1 in [(0,1),(1,2),(2,4)]:
             w_codes = keep.tile([P, (t1 - t0) * P], U32, name=f"w_codes{t0}", align_bytes=64)
             w_bytes = keep.tile([P, (t1 - t0) * P], U8, name=f"w_bytes{t0}", align_bytes=64)
@@ -73,12 +79,13 @@ def tile_picked_sidegate_sigmoid_po_kernel(tc, x_words, x_scales, side, w1, offs
                                   in_=w_bf[:, t0:t1, :, :].rearrange("p t m j -> p (t m j)"))
             for t in range(t0, t1):
                 cols = slice((t - t0) * P, (t - t0 + 1) * P)
-                nc.tensor.matmul_mx(out=acc[t][:], lhsT=w_codes[:, cols].bitcast(FP8X4), lhsT_scale=w_bytes[:, cols],
-                                    rhs=x_codes[:].bitcast(FP8X4), rhs_scale=x_bytes[:], start=True, stop=True)
+                for a, b in spans[t]:
+                    nc.tensor.matmul_mx(out=product(t, a, b), lhsT=w_codes[:, cols].bitcast(FP8X4), lhsT_scale=w_bytes[:, cols],
+                                        rhs=x_codes[:, a:b].bitcast(FP8X4), rhs_scale=x_bytes[:, a:b], start=True, stop=True)
 
         y = keep.tile([P, PACK, S], F32, name="y")
         out_rows = out_0.rearrange("(p t) s -> p t s", t=PACK)
-        units = [(0,256),(256,384),(384,512)]
+        units = [(0,128),(128,256),(256,384),(384,512)]
         grouped = {u: keep.tile([P, u[1] - u[0], PACK], BF16, name=f"grouped{u[0]}", align_bytes=64) for u in units}
 
         def part(a, b):
@@ -92,14 +99,14 @@ def tile_picked_sidegate_sigmoid_po_kernel(tc, x_words, x_scales, side, w1, offs
         def gated(t, a, b):
             gate = keep.tile([P, b - a], F32, name=f"gate{t}_{a}")
             nc.scalar.activation(gate[:], side_all[t][:].indirect(offsets[:, a // 16 : b // 16]), SIGMOID)
-            nc.vector.tensor_tensor(y[:, t, a:b], acc[t][:, a:b], gate[:], MULT)
+            nc.vector.tensor_tensor(y[:, t, a:b], product(t, a, b), gate[:], MULT)
 
         def gated_by_vector(t, a, b):
             picked = keep.tile([P, b - a], F32, name=f"picked{t}_{a}")
             gate = keep.tile([P, b - a], F32, name=f"gate{t}_{a}")
             nc.vector.tensor_copy(picked[:], side_all[t][:].indirect(offsets[:, a // 16 : b // 16]))
             nc.scalar.activation(gate[:], picked[:], SIGMOID)
-            nc.vector.tensor_tensor(y[:, t, a:b], acc[t][:, a:b], gate[:], MULT)
+            nc.vector.tensor_tensor(y[:, t, a:b], product(t, a, b), gate[:], MULT)
 
         def weave(a, b, t0, t1, scalar):
             if t1 - t0 == PACK:
@@ -108,7 +115,9 @@ def tile_picked_sidegate_sigmoid_po_kernel(tc, x_words, x_scales, side, w1, offs
             else:
                 dst = part(a, b)[:, :, t0:t1]
                 src = y[:, t0:t1, a:b].rearrange("p t c -> p c t")
-            if scalar:
+            if scalar == 2:
+                nc.gpsimd.tensor_scalar(dst, src, 1.0, 0.0, MULT, mybir.AluOpType.add)
+            elif scalar:
                 nc.scalar.copy(dst, src)
             else:
                 nc.vector.tensor_copy(dst, src)
@@ -117,11 +126,27 @@ def tile_picked_sidegate_sigmoid_po_kernel(tc, x_words, x_scales, side, w1, offs
             nc.vector.quantize_mx(out=y_codes[:, a:b].bitcast(FP8X4), scales=y_bytes[:, a:b],
                                   in_=part(a, b).rearrange("p c t -> p (c t)"))
 
-        for step in [["g",0,0,256],["g",0,256,512],["g",1,0,256],["w",0,256,0,2,False],["g",1,256,512],["y",0,2],["w",256,384,0,2,False],["w",384,512,0,2,False],["g",2,0,256],["g",2,256,512],["y",2,3],["g",3,0,128],["g",3,128,256],["w",0,256,2,4,False],["g",3,256,384],["q",0,256],["c",0,256],["g",3,384,512],["y",3,4],["w",256,384,2,4,True],["w",384,512,2,4,False],["q",384,512],["q",256,384],["c",256,512]]:
+        gates = [keep.tile([P, S], F32, name=f"gate{t}") for t in range(PACK)]
+        picked = {}
+
+        for step in [["g",0,0,256],["g",0,256,512],["g",1,0,256],["w",0,128,0,2,False],["w",128,256,0,2,False],["g",1,256,512],["y",0,2],["w",256,384,0,2,False],["w",384,512,0,2,False],["g",2,0,256],["g",2,256,512],["y",2,3],["G",3,0,128],["G",3,128,256],["G",3,256,384],["G",3,384,512],["m",3,0,128],["m",3,128,256],["w",0,128,2,4,False],["m",3,256,384],["w",256,384,2,4,True],["w",128,256,2,4,False],["m",3,384,512],["y",3,4],["q",0,128],["w",384,512,2,4,False],["q",128,256],["c",0,256],["q",256,384],["q",384,512],["c",256,512]]:
             if step[0] == "g":
                 gated(step[1], step[2], step[3])
             elif step[0] == "v":
                 gated_by_vector(step[1], step[2], step[3])
+            elif step[0] == "G":
+                t, a, b = step[1:]
+                nc.scalar.activation(gates[t][:, a:b], side_all[t][:].indirect(offsets[:, a // 16 : b // 16]), SIGMOID)
+            elif step[0] == "p":
+                t, a, b = step[1:]
+                picked[t] = keep.tile([P, b - a], F32, name=f"picked{t}") if t < 2 else gates[t - 2][:, a:b]
+                nc.vector.tensor_copy(picked[t][:], side_all[t][:].indirect(offsets[:, a // 16 : b // 16]))
+            elif step[0] == "z":
+                t, a, b = step[1:]
+                nc.scalar.activation(gates[t][:, a:b], picked[t][:], SIGMOID)
+            elif step[0] == "m":
+                t, a, b = step[1:]
+                nc.vector.tensor_tensor(y[:, t, a:b], product(t, a, b), gates[t][:, a:b], MULT)
             elif step[0] == "w":
                 weave(step[1], step[2], step[3], step[4], step[5])
             elif step[0] == "q":

@@ -16,8 +16,8 @@ MULT = mybir.AluOpType.mult
 P = 128
 PACK = 4
 HALF = S // 2
+QUARTER = S // 4
 M_VECTOR = 80
-PRE = True
 
 
 def tile_picked_sidegate_sigmoid_po_kernel(tc, x_words, x_scales, side, w1, offs, out_0, out_1, out_2):
@@ -36,23 +36,13 @@ def tile_picked_sidegate_sigmoid_po_kernel(tc, x_words, x_scales, side, w1, offs
         nc.scalar.activation(warm_out[:], warm[:], SIGMOID)
 
         side_rows = side.rearrange("(p t) c -> p t c", t=PACK)
-
-        def load(what):
-            if what == "x":
-                nc.sync.dma_start(words_all[:], x_words[0].rearrange("p c r -> p (c r)").bitcast(I32))
-            elif what == "o":
-                nc.sync.dma_start(offsets[:], offs)
-            elif what == "b":
-                for q in range(4):
-                    nc.sync.dma_start(scales_all[32 * q : 32 * q + 4, :].bitcast(I32), x_scales[0, 4 * q : 4 * q + 4, :].bitcast(I32))
-            elif what == "w":
-                nc.sync.dma_start(w_raw[:], w1.rearrange("(p j) c -> p j c", j=PACK))
-            else:
-                t = int(what[1])
-                nc.sync.dma_start(side_all[t][:], side_rows[:, t, :])
-
-        for what in ["x","o","b","w","s0","s1","s2","s3"]:
-            load(what)
+        nc.sync.dma_start(words_all[:], x_words[0].rearrange("p c r -> p (c r)").bitcast(I32))
+        nc.sync.dma_start(offsets[:], offs)
+        for q in range(4):
+            nc.sync.dma_start(scales_all[32 * q : 32 * q + 4, :].bitcast(I32), x_scales[0, 4 * q : 4 * q + 4, :].bitcast(I32))
+        nc.sync.dma_start(w_raw[:], w1.rearrange("(p j) c -> p j c", j=PACK))
+        for t in range(PACK):
+            nc.sync.dma_start(side_all[t][:], side_rows[:, t, :])
 
         x_codes = keep.tile([P, S], U32, name="x_codes", align_bytes=64)
         nc.vector.tensor_copy(x_codes[:], words_all[:].bitcast(U32).indirect(offsets[:]))
@@ -72,7 +62,7 @@ def tile_picked_sidegate_sigmoid_po_kernel(tc, x_words, x_scales, side, w1, offs
             u = [u for u in spans[t] if u[0] <= a and b <= u[1]][0]
             return banks[t, u][:, a - u[0] : b - u[0]]
 
-        for t0, t1 in [(0,1),(1,2),(2,4)]:
+        for t0, t1 in [(0, 1), (1, 2), (2, 4)]:
             w_codes = keep.tile([P, (t1 - t0) * P], U32, name=f"w_codes{t0}", align_bytes=64)
             w_bytes = keep.tile([P, (t1 - t0) * P], U8, name=f"w_bytes{t0}", align_bytes=64)
             nc.vector.quantize_mx(out=w_codes[:].bitcast(FP8X4), scales=w_bytes[:],
@@ -85,76 +75,66 @@ def tile_picked_sidegate_sigmoid_po_kernel(tc, x_words, x_scales, side, w1, offs
 
         y = keep.tile([P, PACK, S], F32, name="y")
         out_rows = out_0.rearrange("(p t) s -> p t s", t=PACK)
-        units = [(0,128),(128,256),(256,384),(384,512)]
+        units = [(a, a + QUARTER) for a in range(0, S, QUARTER)]
         grouped = {u: keep.tile([P, u[1] - u[0], PACK], BF16, name=f"grouped{u[0]}", align_bytes=64) for u in units}
-
-        def part(a, b):
-            u = [u for u in units if u[0] <= a and b <= u[1]][0]
-            return grouped[u][:, a - u[0] : b - u[0], :]
-
         y_codes = keep.tile([P, S], U32, name="y_codes", align_bytes=64)
         y_bytes = keep.tile([P, S], U8, name="y_bytes", align_bytes=64)
         words_out = out_1[0].rearrange("p c r -> p (c r)").bitcast(I32)
+        gates = {}
 
-        def gated(t, a, b):
-            gate = keep.tile([P, b - a], F32, name=f"gate{t}_{a}")
-            nc.scalar.activation(gate[:], side_all[t][:].indirect(offsets[:, a // 16 : b // 16]), SIGMOID)
-            nc.vector.tensor_tensor(y[:, t, a:b], product(t, a, b), gate[:], MULT)
+        def look_up(t, a, b):
+            gates[t, a] = keep.tile([P, b - a], F32, name=f"gate{t}_{a}")
+            nc.scalar.activation(gates[t, a][:], side_all[t][:].indirect(offsets[:, a // 16 : b // 16]), SIGMOID)
 
-        def gated_by_vector(t, a, b):
-            picked = keep.tile([P, b - a], F32, name=f"picked{t}_{a}")
-            gate = keep.tile([P, b - a], F32, name=f"gate{t}_{a}")
-            nc.vector.tensor_copy(picked[:], side_all[t][:].indirect(offsets[:, a // 16 : b // 16]))
-            nc.scalar.activation(gate[:], picked[:], SIGMOID)
-            nc.vector.tensor_tensor(y[:, t, a:b], product(t, a, b), gate[:], MULT)
+        def multiply(t, a, b):
+            nc.vector.tensor_tensor(y[:, t, a:b], product(t, a, b), gates[t, a][:], MULT)
 
-        def weave(a, b, t0, t1, scalar):
+        def weave(u, t0, t1, copy):
+            a, b = u
             if t1 - t0 == PACK:
-                dst = part(a, b).rearrange("p (c i) t -> p c t i", i=4)
-                src = y[:, :, a:b].rearrange("p t (c i) -> p c t i", i=4)
+                copy(grouped[u][:].rearrange("p (c i) t -> p c t i", i=4), y[:, :, a:b].rearrange("p t (c i) -> p c t i", i=4))
             else:
-                dst = part(a, b)[:, :, t0:t1]
-                src = y[:, t0:t1, a:b].rearrange("p t c -> p c t")
-            if scalar == 2:
-                nc.gpsimd.tensor_scalar(dst, src, 1.0, 0.0, MULT, mybir.AluOpType.add)
-            elif scalar:
-                nc.scalar.copy(dst, src)
-            else:
-                nc.vector.tensor_copy(dst, src)
+                copy(grouped[u][:, :, t0:t1], y[:, t0:t1, a:b].rearrange("p t c -> p c t"))
 
-        def quantise(a, b):
+        def quantise(u):
+            a, b = u
             nc.vector.quantize_mx(out=y_codes[:, a:b].bitcast(FP8X4), scales=y_bytes[:, a:b],
-                                  in_=part(a, b).rearrange("p c t -> p (c t)"))
+                                  in_=grouped[u][:].rearrange("p c t -> p (c t)"))
 
-        gates = [keep.tile([P, S], F32, name=f"gate{t}") for t in range(PACK)]
-        picked = {}
+        def store_rows(t0, t1):
+            nc.sync.dma_start(out_rows[:, t0:t1, :], y[:, t0:t1, :])
 
-        for step in [["g",0,0,256],["g",0,256,512],["g",1,0,256],["w",0,128,0,2,False],["w",128,256,0,2,False],["g",1,256,512],["y",0,2],["w",256,384,0,2,False],["w",384,512,0,2,False],["g",2,0,256],["g",2,256,512],["y",2,3],["G",3,0,128],["G",3,128,256],["G",3,256,384],["G",3,384,512],["m",3,0,128],["m",3,128,256],["w",0,128,2,4,False],["m",3,256,384],["w",256,384,2,4,True],["w",128,256,2,4,False],["m",3,384,512],["y",3,4],["q",0,128],["w",384,512,2,4,False],["q",128,256],["c",0,256],["q",256,384],["q",384,512],["c",256,512]]:
-            if step[0] == "g":
-                gated(step[1], step[2], step[3])
-            elif step[0] == "v":
-                gated_by_vector(step[1], step[2], step[3])
-            elif step[0] == "G":
-                t, a, b = step[1:]
-                nc.scalar.activation(gates[t][:, a:b], side_all[t][:].indirect(offsets[:, a // 16 : b // 16]), SIGMOID)
-            elif step[0] == "p":
-                t, a, b = step[1:]
-                picked[t] = keep.tile([P, b - a], F32, name=f"picked{t}") if t < 2 else gates[t - 2][:, a:b]
-                nc.vector.tensor_copy(picked[t][:], side_all[t][:].indirect(offsets[:, a // 16 : b // 16]))
-            elif step[0] == "z":
-                t, a, b = step[1:]
-                nc.scalar.activation(gates[t][:, a:b], picked[t][:], SIGMOID)
-            elif step[0] == "m":
-                t, a, b = step[1:]
-                nc.vector.tensor_tensor(y[:, t, a:b], product(t, a, b), gates[t][:, a:b], MULT)
-            elif step[0] == "w":
-                weave(step[1], step[2], step[3], step[4], step[5])
-            elif step[0] == "q":
-                quantise(step[1], step[2])
-            elif step[0] == "y":
-                nc.sync.dma_start(out_rows[:, step[1] : step[2], :], y[:, step[1] : step[2], :])
-            elif step[0] == "c":
-                nc.sync.dma_start(words_out[:, step[1] : step[2]], y_codes[:, step[1] : step[2]].bitcast(I32))
+        def store_words(a, b):
+            nc.sync.dma_start(words_out[:, a:b], y_codes[:, a:b].bitcast(I32))
+
+        by_vector, by_scalar = nc.vector.tensor_copy, nc.scalar.copy
+        for t in range(PACK - 1):
+            for h in range(2):
+                look_up(t, h * HALF, (h + 1) * HALF)
+                multiply(t, h * HALF, (h + 1) * HALF)
+            if t == 1:
+                store_rows(0, 2)
+        store_rows(2, 3)
+
+        for u in units:
+            look_up(3, *u)
+        ua, ub, uc, ud = units
+        multiply(3, *ua)
+        multiply(3, *ub)
+        weave(ua, 0, 4, by_vector)
+        multiply(3, *uc)
+        weave(uc, 0, 4, by_scalar)
+        multiply(3, *ud)
+        store_rows(3, 4)
+        weave(ub, 0, 4, by_vector)
+        quantise(ua)
+        weave(ud, 0, 4, by_vector)
+        quantise(ub)
+        store_words(0, HALF)
+        quantise(uc)
+        quantise(ud)
+        store_words(HALF, S)
+
         for q in range(4):
             queue = nc.scalar if q % 2 == 0 else nc.sync
             queue.dma_start(out_2[0, 4 * q : 4 * q + 4, :].bitcast(I32), y_bytes[32 * q : 32 * q + 4, :].bitcast(I32))

@@ -89,12 +89,13 @@ def tile_picked_sidegate_sigmoid_po_kernel(tc, x_words, x_scales, side, w1, offs
         def multiply(t, a, b):
             nc.vector.tensor_tensor(y[:, t, a:b], product(t, a, b), gates[t, a][:], MULT)
 
-        def weave(u, t0, t1, copy):
-            a, b = u
+        def weave(u, t0, t1, copy, c0=0, c1=QUARTER):
+            a = u[0]
             if t1 - t0 == PACK:
-                copy(grouped[u][:].rearrange("p (c i) t -> p c t i", i=4), y[:, :, a:b].rearrange("p t (c i) -> p c t i", i=4))
+                copy(grouped[u][:, c0:c1, :].rearrange("p (c i) t -> p c t i", i=4),
+                     y[:, :, a + c0 : a + c1].rearrange("p t (c i) -> p c t i", i=4))
             else:
-                copy(grouped[u][:, :, t0:t1], y[:, t0:t1, a:b].rearrange("p t c -> p c t"))
+                copy(grouped[u][:, c0:c1, t0:t1], y[:, t0:t1, a + c0 : a + c1].rearrange("p t c -> p c t"))
 
         def quantise(u):
             a, b = u
@@ -108,27 +109,38 @@ def tile_picked_sidegate_sigmoid_po_kernel(tc, x_words, x_scales, side, w1, offs
             nc.sync.dma_start(words_out[:, a:b], y_codes[:, a:b].bitcast(I32))
 
         by_vector, by_scalar = nc.vector.tensor_copy, nc.scalar.copy
-        for t in range(PACK - 1):
-            for h in range(2):
-                look_up(t, h * HALF, (h + 1) * HALF)
-                multiply(t, h * HALF, (h + 1) * HALF)
-            if t == 1:
-                store_rows(0, 2)
+        ua, ub, uc, ud = units
+        for a, b in spans[0]:
+            look_up(0, a, b)
+            multiply(0, a, b)
+        look_up(1, 0, HALF)
+        multiply(1, 0, HALF)
+        look_up(1, HALF, S)
+        weave(ua, 0, 2, by_vector)
+        multiply(1, HALF, S)
+        store_rows(0, 2)
+        look_up(2, 0, HALF)
+        look_up(2, HALF, S)
+        multiply(2, 0, HALF)
+        weave(uc, 0, 2, by_vector)
+        weave(ud, 0, 2, by_vector, 0, QUARTER // 2)
+        multiply(2, HALF, S)
         store_rows(2, 3)
 
         for u in units:
             look_up(3, *u)
-        ua, ub, uc, ud = units
         multiply(3, *ua)
         multiply(3, *ub)
-        weave(ua, 0, 4, by_vector)
+        weave(ub, 0, 4, by_scalar)
+        nc.sync.dma_start(out_rows[:, 3, :HALF], y[:, 3, :HALF])
+        weave(ua, 2, 4, by_vector)
         multiply(3, *uc)
-        weave(uc, 0, 4, by_scalar)
         multiply(3, *ud)
-        store_rows(3, 4)
-        weave(ub, 0, 4, by_vector)
+        weave(ud, 0, 4, by_scalar, QUARTER // 2, QUARTER)
+        nc.sync.dma_start(out_rows[:, 3, HALF:], y[:, 3, HALF:])
+        weave(uc, 2, 4, by_vector)
         quantise(ua)
-        weave(ud, 0, 4, by_vector)
+        weave(ud, 2, 4, by_vector, 0, QUARTER // 2)
         quantise(ub)
         store_words(0, HALF)
         quantise(uc)

@@ -40,14 +40,24 @@ def tile_picked_sidegate_sigmoid_po_kernel(tc, x_words, x_scales, side, w1, offs
         nc.sync.dma_start(offsets[:], offs)
         for q in range(4):
             nc.sync.dma_start(scales_all[32 * q : 32 * q + 4, :].bitcast(I32), x_scales[0, 4 * q : 4 * q + 4, :].bitcast(I32))
+        nc.sync.dma_start(side_all[0][:], side_rows[:, 0, :])
         nc.sync.dma_start(w_raw[:], w1.rearrange("(p j) c -> p j c", j=PACK))
-        for t in range(PACK):
+        for t in range(1, PACK):
             nc.sync.dma_start(side_all[t][:], side_rows[:, t, :])
 
         x_codes = keep.tile([P, S], U32, name="x_codes", align_bytes=64)
         nc.vector.tensor_copy(x_codes[:], words_all[:].bitcast(U32).indirect(offsets[:]))
         x_bytes = keep.tile([P, S], U8, name="x_bytes", align_bytes=64)
         nc.vector.tensor_copy(x_bytes[:], scales_all[:].indirect(offsets[:]))
+
+        gates = {}
+
+        def look_up(t, a, b):
+            gates[t, a] = keep.tile([P, b - a], F32, name=f"gate{t}_{a}")
+            nc.scalar.activation(gates[t, a][:], side_all[t][:].indirect(offsets[:, a // 16 : b // 16]), SIGMOID)
+
+        for h in range(2):
+            look_up(0, h * HALF, (h + 1) * HALF)
 
         w_bf = keep.tile([P, PACK, P, PACK], BF16, name="w_bf", align_bytes=64)
         w_dst = w_bf[:].rearrange("p t m j -> p m j t")
@@ -80,11 +90,6 @@ def tile_picked_sidegate_sigmoid_po_kernel(tc, x_words, x_scales, side, w1, offs
         y_codes = keep.tile([P, S], U32, name="y_codes", align_bytes=64)
         y_bytes = keep.tile([P, S], U8, name="y_bytes", align_bytes=64)
         words_out = out_1[0].rearrange("p c r -> p (c r)").bitcast(I32)
-        gates = {}
-
-        def look_up(t, a, b):
-            gates[t, a] = keep.tile([P, b - a], F32, name=f"gate{t}_{a}")
-            nc.scalar.activation(gates[t, a][:], side_all[t][:].indirect(offsets[:, a // 16 : b // 16]), SIGMOID)
 
         def multiply(t, a, b):
             nc.vector.tensor_tensor(y[:, t, a:b], product(t, a, b), gates[t, a][:], MULT)
@@ -111,7 +116,6 @@ def tile_picked_sidegate_sigmoid_po_kernel(tc, x_words, x_scales, side, w1, offs
         by_vector, by_scalar = nc.vector.tensor_copy, nc.scalar.copy
         ua, ub, uc, ud = units
         for a, b in spans[0]:
-            look_up(0, a, b)
             multiply(0, a, b)
         look_up(1, 0, HALF)
         multiply(1, 0, HALF)
@@ -122,29 +126,28 @@ def tile_picked_sidegate_sigmoid_po_kernel(tc, x_words, x_scales, side, w1, offs
         look_up(2, 0, HALF)
         look_up(2, HALF, S)
         multiply(2, 0, HALF)
-        weave(uc, 0, 2, by_vector)
-        weave(ud, 0, 2, by_vector, 0, QUARTER // 2)
+        weave(ub, 0, 2, by_vector)
+        weave(uc, 0, 2, by_vector, 0, QUARTER // 2)
         multiply(2, HALF, S)
         store_rows(2, 3)
 
-        for u in units:
+        for u in (ua, ud, ub, uc):
             look_up(3, *u)
         multiply(3, *ua)
-        multiply(3, *ub)
-        weave(ub, 0, 4, by_scalar)
-        nc.sync.dma_start(out_rows[:, 3, :HALF], y[:, 3, :HALF])
-        weave(ua, 2, 4, by_vector)
-        multiply(3, *uc)
         multiply(3, *ud)
-        weave(ud, 0, 4, by_scalar, QUARTER // 2, QUARTER)
-        nc.sync.dma_start(out_rows[:, 3, HALF:], y[:, 3, HALF:])
-        weave(uc, 2, 4, by_vector)
+        weave(ud, 0, 4, by_scalar)
+        weave(ua, 2, 4, by_vector)
+        multiply(3, *ub)
+        multiply(3, *uc)
+        weave(uc, 0, 4, by_scalar, QUARTER // 2, QUARTER)
+        store_rows(3, 4)
+        weave(ub, 2, 4, by_vector)
         quantise(ua)
-        weave(ud, 2, 4, by_vector, 0, QUARTER // 2)
+        weave(uc, 2, 4, by_vector, 0, QUARTER // 2)
         quantise(ub)
         store_words(0, HALF)
-        quantise(uc)
         quantise(ud)
+        quantise(uc)
         store_words(HALF, S)
 
         for q in range(4):

@@ -15,9 +15,11 @@ MULT = mybir.AluOpType.mult
 
 P = 128
 PACK = 4
+QUADRANTS = 4
 HALF = S // 2
 QUARTER = S // 4
-M_VECTOR = 80
+EIGHTH = S // 8
+M_VECTOR = 32
 
 
 def tile_picked_sidegate_sigmoid_po_kernel(tc, x_words, x_scales, side, w1, offs, out_0, out_1, out_2):
@@ -38,7 +40,7 @@ def tile_picked_sidegate_sigmoid_po_kernel(tc, x_words, x_scales, side, w1, offs
         side_rows = side.rearrange("(p t) c -> p t c", t=PACK)
         nc.sync.dma_start(words_all[:], x_words[0].rearrange("p c r -> p (c r)").bitcast(I32))
         nc.sync.dma_start(offsets[:], offs)
-        for q in range(4):
+        for q in range(QUADRANTS):
             nc.sync.dma_start(scales_all[32 * q : 32 * q + 4, :].bitcast(I32), x_scales[0, 4 * q : 4 * q + 4, :].bitcast(I32))
         nc.sync.dma_start(side_all[0][:], side_rows[:, 0, :])
         nc.sync.dma_start(w_raw[:], w1.rearrange("(p j) c -> p j c", j=PACK))
@@ -56,21 +58,23 @@ def tile_picked_sidegate_sigmoid_po_kernel(tc, x_words, x_scales, side, w1, offs
             gates[t, a] = keep.tile([P, b - a], F32, name=f"gate{t}_{a}")
             nc.scalar.activation(gates[t, a][:], side_all[t][:].indirect(offsets[:, a // 16 : b // 16]), SIGMOID)
 
-        for h in range(2):
-            look_up(0, h * HALF, (h + 1) * HALF)
+        halves = [(0, HALF), (HALF, S)]
+        for a, b in halves:
+            look_up(0, a, b)
 
         w_bf = keep.tile([P, PACK, P, PACK], BF16, name="w_bf", align_bytes=64)
         w_dst = w_bf[:].rearrange("p t m j -> p m j t")
         w_src = w_raw[:].rearrange("p j (m t) -> p m j t", t=PACK)
-        nc.vector.tensor_copy(w_dst[:, :M_VECTOR], w_src[:, :M_VECTOR])
-        nc.scalar.copy(w_dst[:, M_VECTOR:], w_src[:, M_VECTOR:])
+        nc.vector.tensor_copy(w_dst[:, :, :, :2], w_src[:, :, :, :2])
+        nc.vector.tensor_copy(w_dst[:, :M_VECTOR, :, 2:], w_src[:, :M_VECTOR, :, 2:])
+        nc.scalar.copy(w_dst[:, M_VECTOR:, :, 2:], w_src[:, M_VECTOR:, :, 2:])
 
-        spans = {t: [(0, HALF), (HALF, S)] if t == 0 else [(0, S)] for t in range(PACK)}
-        banks = {(t, u): psum.tile([P, u[1] - u[0]], F32, name=f"acc{t}_{u[0]}") for t in range(PACK) for u in spans[t]}
+        spans = {t: halves if t == 0 else [(0, S)] for t in range(PACK)}
+        banks = {(t, span): psum.tile([P, span[1] - span[0]], F32, name=f"acc{t}_{span[0]}") for t in range(PACK) for span in spans[t]}
 
         def product(t, a, b):
-            u = [u for u in spans[t] if u[0] <= a and b <= u[1]][0]
-            return banks[t, u][:, a - u[0] : b - u[0]]
+            span = [span for span in spans[t] if span[0] <= a and b <= span[1]][0]
+            return banks[t, span][:, a - span[0] : b - span[0]]
 
         for t0, t1 in [(0, 1), (1, 2), (2, 4)]:
             w_codes = keep.tile([P, (t1 - t0) * P], U32, name=f"w_codes{t0}", align_bytes=64)
@@ -84,9 +88,9 @@ def tile_picked_sidegate_sigmoid_po_kernel(tc, x_words, x_scales, side, w1, offs
                                         rhs=x_codes[:, a:b].bitcast(FP8X4), rhs_scale=x_bytes[:, a:b], start=True, stop=True)
 
         y = keep.tile([P, PACK, S], F32, name="y")
-        out_rows = out_0.rearrange("(p t) s -> p t s", t=PACK)
-        units = [(a, a + QUARTER) for a in range(0, S, QUARTER)]
-        grouped = {u: keep.tile([P, u[1] - u[0], PACK], BF16, name=f"grouped{u[0]}", align_bytes=64) for u in units}
+        out_rows = out_0.rearrange("(p t) s -> p (t s)", t=PACK)
+        quarters = [(a, a + QUARTER) for a in range(0, S, QUARTER)]
+        woven = {u: keep.tile([P, QUARTER, PACK], BF16, name=f"woven{u[0]}", align_bytes=64) for u in quarters}
         y_codes = keep.tile([P, S], U32, name="y_codes", align_bytes=64)
         y_bytes = keep.tile([P, S], U8, name="y_bytes", align_bytes=64)
         words_out = out_1[0].rearrange("p c r -> p (c r)").bitcast(I32)
@@ -94,62 +98,66 @@ def tile_picked_sidegate_sigmoid_po_kernel(tc, x_words, x_scales, side, w1, offs
         def multiply(t, a, b):
             nc.vector.tensor_tensor(y[:, t, a:b], product(t, a, b), gates[t, a][:], MULT)
 
-        def weave(u, t0, t1, copy, c0=0, c1=QUARTER):
-            a = u[0]
-            if t1 - t0 == PACK:
-                copy(grouped[u][:, c0:c1, :].rearrange("p (c i) t -> p c t i", i=4),
-                     y[:, :, a + c0 : a + c1].rearrange("p t (c i) -> p c t i", i=4))
-            else:
-                copy(grouped[u][:, c0:c1, t0:t1], y[:, t0:t1, a + c0 : a + c1].rearrange("p t c -> p c t"))
+        def weave_pair(u, t, width):
+            nc.vector.tensor_copy(woven[u][:, :width, t : t + 2], y[:, t : t + 2, u[0] : u[0] + width].rearrange("p t c -> p c t"))
+
+        def weave_whole(u, first):
+            nc.scalar.copy(woven[u][:, first:, :].rearrange("p (c i) t -> p c t i", i=4),
+                           y[:, :, u[0] + first : u[1]].rearrange("p t (c i) -> p c t i", i=4))
 
         def quantise(u):
             a, b = u
             nc.vector.quantize_mx(out=y_codes[:, a:b].bitcast(FP8X4), scales=y_bytes[:, a:b],
-                                  in_=grouped[u][:].rearrange("p c t -> p (c t)"))
+                                  in_=woven[u][:].rearrange("p c t -> p (c t)"))
 
-        def store_rows(t0, t1):
-            nc.sync.dma_start(out_rows[:, t0:t1, :], y[:, t0:t1, :])
+        def store_rows(a, b):
+            nc.sync.dma_start(out_rows[:, a:b], y[:].rearrange("p t s -> p (t s)")[:, a:b])
 
         def store_words(a, b):
             nc.sync.dma_start(words_out[:, a:b], y_codes[:, a:b].bitcast(I32))
 
-        by_vector, by_scalar = nc.vector.tensor_copy, nc.scalar.copy
-        ua, ub, uc, ud = units
-        for a, b in spans[0]:
+        first, second, third, fourth = quarters
+
+        picked = keep.tile([P, QUARTER], F32, name="picked")
+        nc.vector.tensor_copy(picked[:], side_all[1][:].indirect(offsets[:, fourth[0] // 16 :]))
+        for a, b in halves:
             multiply(0, a, b)
         look_up(1, 0, HALF)
         multiply(1, 0, HALF)
-        look_up(1, HALF, S)
-        weave(ua, 0, 2, by_vector)
-        multiply(1, HALF, S)
-        store_rows(0, 2)
-        look_up(2, 0, HALF)
-        look_up(2, HALF, S)
+        store_rows(0, S + HALF)
+        look_up(1, *third)
+        gates[1, fourth[0]] = keep.tile([P, QUARTER], F32, name="gate_of_picked")
+        nc.scalar.activation(gates[1, fourth[0]][:], picked[:], SIGMOID)
+        weave_pair(first, 0, QUARTER)
+        multiply(1, *third)
+        multiply(1, *fourth)
+        for a, b in halves:
+            look_up(2, a, b)
         multiply(2, 0, HALF)
-        weave(ub, 0, 2, by_vector)
-        weave(uc, 0, 2, by_vector, 0, QUARTER // 2)
+        weave_pair(second, 0, QUARTER)
+        weave_pair(third, 0, EIGHTH)
         multiply(2, HALF, S)
-        store_rows(2, 3)
+        store_rows(S + HALF, 3 * S)
 
-        for u in (ua, ud, ub, uc):
+        for u in (first, fourth, second, third):
             look_up(3, *u)
-        multiply(3, *ua)
-        multiply(3, *ud)
-        weave(ud, 0, 4, by_scalar)
-        weave(ua, 2, 4, by_vector)
-        multiply(3, *ub)
-        multiply(3, *uc)
-        weave(uc, 0, 4, by_scalar, QUARTER // 2, QUARTER)
-        store_rows(3, 4)
-        weave(ub, 2, 4, by_vector)
-        quantise(ua)
-        weave(uc, 2, 4, by_vector, 0, QUARTER // 2)
-        quantise(ub)
+        multiply(3, *first)
+        multiply(3, *fourth)
+        weave_whole(fourth, 0)
+        weave_pair(first, 2, QUARTER)
+        multiply(3, *second)
+        multiply(3, *third)
+        weave_whole(third, EIGHTH)
+        store_rows(3 * S, 4 * S)
+        weave_pair(second, 2, QUARTER)
+        quantise(first)
+        weave_pair(third, 2, EIGHTH)
+        quantise(second)
         store_words(0, HALF)
-        quantise(ud)
-        quantise(uc)
+        quantise(fourth)
+        quantise(third)
         store_words(HALF, S)
 
-        for q in range(4):
+        for q in range(QUADRANTS):
             queue = nc.scalar if q % 2 == 0 else nc.sync
             queue.dma_start(out_2[0, 4 * q : 4 * q + 4, :].bitcast(I32), y_bytes[32 * q : 32 * q + 4, :].bitcast(I32))

@@ -19,7 +19,7 @@ QUADRANTS = 4
 HALF = S // 2
 QUARTER = S // 4
 EIGHTH = S // 8
-M_VECTOR = 32
+PICKED = 192
 
 
 def tile_picked_sidegate_sigmoid_po_kernel(tc, x_words, x_scales, side, w1, offs, out_0, out_1, out_2):
@@ -66,8 +66,7 @@ def tile_picked_sidegate_sigmoid_po_kernel(tc, x_words, x_scales, side, w1, offs
         w_dst = w_bf[:].rearrange("p t m j -> p m j t")
         w_src = w_raw[:].rearrange("p j (m t) -> p m j t", t=PACK)
         nc.vector.tensor_copy(w_dst[:, :, :, :2], w_src[:, :, :, :2])
-        nc.vector.tensor_copy(w_dst[:, :M_VECTOR, :, 2:], w_src[:, :M_VECTOR, :, 2:])
-        nc.scalar.copy(w_dst[:, M_VECTOR:, :, 2:], w_src[:, M_VECTOR:, :, 2:])
+        nc.scalar.copy(w_dst[:, :, :, 2:], w_src[:, :, :, 2:])
 
         spans = {t: halves if t == 0 else [(0, S)] for t in range(PACK)}
         banks = {(t, span): psum.tile([P, span[1] - span[0]], F32, name=f"acc{t}_{span[0]}") for t in range(PACK) for span in spans[t]}
@@ -118,25 +117,22 @@ def tile_picked_sidegate_sigmoid_po_kernel(tc, x_words, x_scales, side, w1, offs
 
         first, second, third, fourth = quarters
 
-        picked = keep.tile([P, QUARTER], F32, name="picked")
-        nc.vector.tensor_copy(picked[:], side_all[1][:].indirect(offsets[:, fourth[0] // 16 :]))
+        own = S - PICKED
+        picked = keep.tile([P, PICKED], F32, name="picked")
+        nc.vector.tensor_copy(picked[:], side_all[1][:].indirect(offsets[:, own // 16 :]))
         for a, b in halves:
             multiply(0, a, b)
-        look_up(1, 0, HALF)
-        multiply(1, 0, HALF)
+        look_up(1, 0, own)
+        multiply(1, 0, own)
         store_rows(0, S + HALF)
-        look_up(1, *third)
-        gates[1, fourth[0]] = keep.tile([P, QUARTER], F32, name="gate_of_picked")
-        nc.scalar.activation(gates[1, fourth[0]][:], picked[:], SIGMOID)
+        gates[1, own] = keep.tile([P, PICKED], F32, name="gate_of_picked")
+        nc.scalar.activation(gates[1, own][:], picked[:], SIGMOID)
         weave_pair(first, 0, QUARTER)
-        multiply(1, *third)
-        multiply(1, *fourth)
-        for a, b in halves:
-            look_up(2, a, b)
-        multiply(2, 0, HALF)
+        multiply(1, own, S)
+        look_up(2, 0, S)
         weave_pair(second, 0, QUARTER)
         weave_pair(third, 0, EIGHTH)
-        multiply(2, HALF, S)
+        multiply(2, 0, S)
         store_rows(S + HALF, 3 * S)
 
         for u in (first, fourth, second, third):

@@ -100,6 +100,9 @@ def tile_picked_sidegate_sigmoid_po_kernel(tc, x_words, x_scales, side, w1, offs
         def weave_pair(u, t, width):
             nc.vector.tensor_copy(woven[u][:, :width, t : t + 2], y[:, t : t + 2, u[0] : u[0] + width].rearrange("p t c -> p c t"))
 
+        def weave_pair_scalar(u):
+            nc.scalar.copy(woven[u][:, :, 2:], y[:, 2:, u[0] : u[1]].rearrange("p t c -> p c t"))
+
         def weave_whole(u, first):
             nc.scalar.copy(woven[u][:, first:, :].rearrange("p (c i) t -> p c t i", i=4),
                            y[:, :, u[0] + first : u[1]].rearrange("p t (c i) -> p c t i", i=4))
@@ -131,27 +134,27 @@ def tile_picked_sidegate_sigmoid_po_kernel(tc, x_words, x_scales, side, w1, offs
         multiply(1, own, S)
         look_up(2, 0, S)
         weave_pair(second, 0, QUARTER)
-        weave_pair(third, 0, EIGHTH)
+        weave_pair(third, 0, QUARTER)
+        weave_pair(fourth, 0, QUARTER)
         multiply(2, 0, S)
         store_rows(S + HALF, 3 * S)
 
-        for u in (first, fourth, second, third):
+        for u in quarters:
             look_up(3, *u)
         multiply(3, *first)
-        multiply(3, *fourth)
-        weave_whole(fourth, 0)
-        weave_pair(first, 2, QUARTER)
         multiply(3, *second)
+        weave_pair_scalar(second)
+        weave_pair(first, 2, QUARTER)
         multiply(3, *third)
-        weave_whole(third, EIGHTH)
+        weave_pair_scalar(third)
+        multiply(3, *fourth)
         store_rows(3 * S, 4 * S)
-        weave_pair(second, 2, QUARTER)
         quantise(first)
-        weave_pair(third, 2, EIGHTH)
+        weave_pair(fourth, 2, QUARTER)
         quantise(second)
         store_words(0, HALF)
-        quantise(fourth)
         quantise(third)
+        quantise(fourth)
         store_words(HALF, S)
 
         for q in range(QUADRANTS):

@@ -12,6 +12,7 @@ U8 = mybir.dt.uint8
 FP8X4 = mybir.dt.float8_e4m3fn_x4
 SIGMOID = mybir.ActivationFunctionType.Sigmoid
 MULT = mybir.AluOpType.mult
+ADD = mybir.AluOpType.add
 
 P = 128
 PACK = 4
@@ -89,7 +90,9 @@ def tile_picked_sidegate_sigmoid_po_kernel(tc, x_words, x_scales, side, w1, offs
         y = keep.tile([P, PACK, S], F32, name="y")
         out_rows = out_0.rearrange("(p t) s -> p (t s)", t=PACK)
         quarters = [(a, a + QUARTER) for a in range(0, S, QUARTER)]
-        woven = {u: keep.tile([P, QUARTER, PACK], BF16, name=f"woven{u[0]}", align_bytes=64) for u in quarters}
+        middle = keep.tile([P, HALF, PACK], BF16, name="woven_middle", align_bytes=64)
+        woven = {u: keep.tile([P, QUARTER, PACK], BF16, name=f"woven{u[0]}", align_bytes=64) for u in (quarters[0], quarters[3])}
+        woven.update({quarters[1]: middle[:, :QUARTER, :], quarters[2]: middle[:, QUARTER:, :]})
         y_codes = keep.tile([P, S], U32, name="y_codes", align_bytes=64)
         y_bytes = keep.tile([P, S], U8, name="y_bytes", align_bytes=64)
         words_out = out_1[0].rearrange("p c r -> p (c r)").bitcast(I32)
@@ -103,6 +106,9 @@ def tile_picked_sidegate_sigmoid_po_kernel(tc, x_words, x_scales, side, w1, offs
         def weave_pair_scalar(u):
             nc.scalar.copy(woven[u][:, :, 2:], y[:, 2:, u[0] : u[1]].rearrange("p t c -> p c t"))
 
+        def weave_early_gpsimd(u):
+            nc.gpsimd.tensor_scalar(woven[u][:, :, :2], y[:, :2, u[0] : u[1]].rearrange("p t c -> p c t"), 1.0, -0.0, MULT, ADD)
+
         def weave_whole(u, first):
             nc.scalar.copy(woven[u][:, first:, :].rearrange("p (c i) t -> p c t i", i=4),
                            y[:, :, u[0] + first : u[1]].rearrange("p t (c i) -> p c t i", i=4))
@@ -110,7 +116,7 @@ def tile_picked_sidegate_sigmoid_po_kernel(tc, x_words, x_scales, side, w1, offs
         def quantise(u):
             a, b = u
             nc.vector.quantize_mx(out=y_codes[:, a:b].bitcast(FP8X4), scales=y_bytes[:, a:b],
-                                  in_=woven[u][:].rearrange("p c t -> p (c t)"))
+                                  in_=woven[u][:, :, :].rearrange("p c t -> p (c t)"))
 
         def store_rows(a, b):
             nc.sync.dma_start(out_rows[:, a:b], y[:].rearrange("p t s -> p (t s)")[:, a:b])
@@ -120,24 +126,26 @@ def tile_picked_sidegate_sigmoid_po_kernel(tc, x_words, x_scales, side, w1, offs
 
         first, second, third, fourth = quarters
 
-        own = S - PICKED
+        pick_end = third[1]
+        pick_start = pick_end - PICKED
         picked = keep.tile([P, PICKED], F32, name="picked")
-        nc.vector.tensor_copy(picked[:], side_all[1][:].indirect(offsets[:, own // 16 :]))
+        nc.vector.tensor_copy(picked[:], side_all[1][:].indirect(offsets[:, pick_start // 16 : pick_end // 16]))
         for a, b in halves:
             multiply(0, a, b)
-        look_up(1, 0, own)
-        multiply(1, 0, own)
-        store_rows(0, S + HALF)
-        gates[1, own] = keep.tile([P, PICKED], F32, name="gate_of_picked")
-        nc.scalar.activation(gates[1, own][:], picked[:], SIGMOID)
+        look_up(1, 0, pick_start)
+        look_up(1, pick_end, S)
+        gates[1, pick_start] = keep.tile([P, PICKED], F32, name="gate_of_picked")
+        nc.scalar.activation(gates[1, pick_start][:], picked[:], SIGMOID)
+        multiply(1, 0, pick_start)
+        store_rows(0, S + pick_start)
+        multiply(1, pick_end, S)
         weave_pair(first, 0, QUARTER)
-        multiply(1, own, S)
-        look_up(2, 0, S)
-        weave_pair(second, 0, QUARTER)
-        weave_pair(third, 0, QUARTER)
         weave_pair(fourth, 0, QUARTER)
+        multiply(1, pick_start, pick_end)
+        nc.gpsimd.tensor_scalar(middle[:, :, :2], y[:, :2, second[0] : third[1]].rearrange("p t c -> p c t"), 1.0, -0.0, MULT, ADD)
+        look_up(2, 0, S)
         multiply(2, 0, S)
-        store_rows(S + HALF, 3 * S)
+        store_rows(S + pick_start, 3 * S)
 
         for u in quarters:
             look_up(3, *u)
@@ -158,5 +166,5 @@ def tile_picked_sidegate_sigmoid_po_kernel(tc, x_words, x_scales, side, w1, offs
         store_words(HALF, S)
 
         for q in range(QUADRANTS):
-            queue = nc.scalar if q % 2 == 0 else nc.sync
+            queue = nc.sync if q == 1 else nc.scalar
             queue.dma_start(out_2[0, 4 * q : 4 * q + 4, :].bitcast(I32), y_bytes[32 * q : 32 * q + 4, :].bitcast(I32))

@@ -19,7 +19,6 @@ PACK = 4
 QUADRANTS = 4
 HALF = S // 2
 QUARTER = S // 4
-EIGHTH = S // 8
 PICKED = 192
 
 
@@ -53,15 +52,12 @@ def tile_picked_sidegate_sigmoid_po_kernel(tc, x_words, x_scales, side, w1, offs
         x_bytes = keep.tile([P, S], U8, name="x_bytes", align_bytes=64)
         nc.vector.tensor_copy(x_bytes[:], scales_all[:].indirect(offsets[:]))
 
-        gates = {}
+        gates = [keep.tile([P, S], F32, name=f"gate{t}") for t in range(PACK)]
 
         def look_up(t, a, b):
-            gates[t, a] = keep.tile([P, b - a], F32, name=f"gate{t}_{a}")
-            nc.scalar.activation(gates[t, a][:], side_all[t][:].indirect(offsets[:, a // 16 : b // 16]), SIGMOID)
+            nc.scalar.activation(gates[t][:, a:b], side_all[t][:].indirect(offsets[:, a // 16 : b // 16]), SIGMOID)
 
-        halves = [(0, HALF), (HALF, S)]
-        for a, b in halves:
-            look_up(0, a, b)
+        look_up(0, 0, S)
 
         w_bf = keep.tile([P, PACK, P, PACK], BF16, name="w_bf", align_bytes=64)
         w_dst = w_bf[:].rearrange("p t m j -> p m j t")
@@ -69,7 +65,7 @@ def tile_picked_sidegate_sigmoid_po_kernel(tc, x_words, x_scales, side, w1, offs
         nc.vector.tensor_copy(w_dst[:, :, :, :2], w_src[:, :, :, :2])
         nc.scalar.copy(w_dst[:, :, :, 2:], w_src[:, :, :, 2:])
 
-        spans = {t: halves if t == 0 else [(0, S)] for t in range(PACK)}
+        spans = {t: [(0, HALF), (HALF, S)] if t == 0 else [(0, S)] for t in range(PACK)}
         banks = {(t, span): psum.tile([P, span[1] - span[0]], F32, name=f"acc{t}_{span[0]}") for t in range(PACK) for span in spans[t]}
 
         def product(t, a, b):
@@ -89,34 +85,20 @@ def tile_picked_sidegate_sigmoid_po_kernel(tc, x_words, x_scales, side, w1, offs
 
         y = keep.tile([P, PACK, S], F32, name="y")
         out_rows = out_0.rearrange("(p t) s -> p (t s)", t=PACK)
-        quarters = [(a, a + QUARTER) for a in range(0, S, QUARTER)]
-        middle = keep.tile([P, HALF, PACK], BF16, name="woven_middle", align_bytes=64)
-        woven = {u: keep.tile([P, QUARTER, PACK], BF16, name=f"woven{u[0]}", align_bytes=64) for u in (quarters[0], quarters[3])}
-        woven.update({quarters[1]: middle[:, :QUARTER, :], quarters[2]: middle[:, QUARTER:, :]})
+        woven = keep.tile([P, S, PACK], BF16, name="woven", align_bytes=64)
         y_codes = keep.tile([P, S], U32, name="y_codes", align_bytes=64)
         y_bytes = keep.tile([P, S], U8, name="y_bytes", align_bytes=64)
         words_out = out_1[0].rearrange("p c r -> p (c r)").bitcast(I32)
 
         def multiply(t, a, b):
-            nc.vector.tensor_tensor(y[:, t, a:b], product(t, a, b), gates[t, a][:], MULT)
+            nc.vector.tensor_tensor(y[:, t, a:b], product(t, a, b), gates[t][:, a:b], MULT)
 
-        def weave_pair(u, t, width):
-            nc.vector.tensor_copy(woven[u][:, :width, t : t + 2], y[:, t : t + 2, u[0] : u[0] + width].rearrange("p t c -> p c t"))
+        def pair(t, a, b):
+            return woven[:, a:b, t : t + 2], y[:, t : t + 2, a:b].rearrange("p t c -> p c t")
 
-        def weave_pair_scalar(u):
-            nc.scalar.copy(woven[u][:, :, 2:], y[:, 2:, u[0] : u[1]].rearrange("p t c -> p c t"))
-
-        def weave_early_gpsimd(u):
-            nc.gpsimd.tensor_scalar(woven[u][:, :, :2], y[:, :2, u[0] : u[1]].rearrange("p t c -> p c t"), 1.0, -0.0, MULT, ADD)
-
-        def weave_whole(u, first):
-            nc.scalar.copy(woven[u][:, first:, :].rearrange("p (c i) t -> p c t i", i=4),
-                           y[:, :, u[0] + first : u[1]].rearrange("p t (c i) -> p c t i", i=4))
-
-        def quantise(u):
-            a, b = u
+        def quantise(a, b):
             nc.vector.quantize_mx(out=y_codes[:, a:b].bitcast(FP8X4), scales=y_bytes[:, a:b],
-                                  in_=woven[u][:, :, :].rearrange("p c t -> p (c t)"))
+                                  in_=woven[:, a:b, :].rearrange("p c t -> p (c t)"))
 
         def store_rows(a, b):
             nc.sync.dma_start(out_rows[:, a:b], y[:].rearrange("p t s -> p (t s)")[:, a:b])
@@ -124,45 +106,47 @@ def tile_picked_sidegate_sigmoid_po_kernel(tc, x_words, x_scales, side, w1, offs
         def store_words(a, b):
             nc.sync.dma_start(words_out[:, a:b], y_codes[:, a:b].bitcast(I32))
 
-        first, second, third, fourth = quarters
+        first, second, third, fourth = [(a, a + QUARTER) for a in range(0, S, QUARTER)]
 
-        pick_end = third[1]
-        pick_start = pick_end - PICKED
+        def weave_gpsimd(t, a, b):
+            dst, src = pair(t, a, b)
+            nc.gpsimd.tensor_scalar(dst, src, 1.0, -0.0, MULT, ADD)
+
         picked = keep.tile([P, PICKED], F32, name="picked")
-        nc.vector.tensor_copy(picked[:], side_all[1][:].indirect(offsets[:, pick_start // 16 : pick_end // 16]))
-        for a, b in halves:
+        nc.vector.tensor_copy(picked[:], side_all[1][:].indirect(offsets[:, (S - PICKED) // 16 :]))
+        for a, b in spans[0]:
             multiply(0, a, b)
-        look_up(1, 0, pick_start)
-        look_up(1, pick_end, S)
-        gates[1, pick_start] = keep.tile([P, PICKED], F32, name="gate_of_picked")
-        nc.scalar.activation(gates[1, pick_start][:], picked[:], SIGMOID)
-        multiply(1, 0, pick_start)
-        store_rows(0, S + pick_start)
-        multiply(1, pick_end, S)
-        weave_pair(first, 0, QUARTER)
-        weave_pair(fourth, 0, QUARTER)
-        multiply(1, pick_start, pick_end)
-        nc.gpsimd.tensor_scalar(middle[:, :, :2], y[:, :2, second[0] : third[1]].rearrange("p t c -> p c t"), 1.0, -0.0, MULT, ADD)
+        look_up(1, 0, PICKED)
+        look_up(1, PICKED, S - PICKED)
+        nc.scalar.activation(gates[1][:, S - PICKED :], picked[:], SIGMOID)
+        multiply(1, 0, PICKED)
+        multiply(1, PICKED, S - PICKED)
+        store_rows(0, 2 * S - PICKED)
+        nc.vector.tensor_copy(*pair(0, *first))
+        multiply(1, *fourth)
+        multiply(1, S - PICKED, third[1])
+        nc.vector.tensor_copy(*pair(0, *fourth))
+        weave_gpsimd(0, second[0], third[1])
         look_up(2, 0, S)
         multiply(2, 0, S)
-        store_rows(S + pick_start, 3 * S)
+        store_rows(2 * S - PICKED, 3 * S)
 
-        for u in quarters:
+        for u in (first, second, third, fourth):
             look_up(3, *u)
         multiply(3, *first)
         multiply(3, *second)
-        weave_pair_scalar(second)
-        weave_pair(first, 2, QUARTER)
+        nc.scalar.copy(*pair(2, *second))
+        nc.vector.tensor_copy(*pair(2, *first))
         multiply(3, *third)
-        weave_pair_scalar(third)
+        nc.scalar.copy(*pair(2, *third))
         multiply(3, *fourth)
         store_rows(3 * S, 4 * S)
-        quantise(first)
-        weave_pair(fourth, 2, QUARTER)
-        quantise(second)
+        quantise(*first)
+        nc.vector.tensor_copy(*pair(2, *fourth))
+        quantise(*second)
         store_words(0, HALF)
-        quantise(third)
-        quantise(fourth)
+        quantise(*third)
+        quantise(*fourth)
         store_words(HALF, S)
 
         for q in range(QUADRANTS):

import concourse.mybir as mybir

K, T, S, N = 512, 1024, 512, 512
FLOPS = 2 * K * S * N

F32 = mybir.dt.float32
BF16 = mybir.dt.bfloat16
I32 = mybir.dt.int32
U32 = mybir.dt.uint32
U16 = mybir.dt.uint16
U8 = mybir.dt.uint8
FP8X4 = mybir.dt.float8_e4m3fn_x4
SIGMOID = mybir.ActivationFunctionType.Sigmoid
MULT = mybir.AluOpType.mult
ADD = mybir.AluOpType.add

P = 128
PACK = 4
QUADRANTS = 4
HALF = S // 2
QUARTER = S // 4
PICKED = 192


def tile_picked_sidegate_sigmoid_po_kernel(tc, x_words, x_scales, side, w1, offs, out_0, out_1, out_2):
    nc = tc.nc
    with tc.tile_pool(name="keep", bufs=1) as keep, tc.psum_pool(name="psum", bufs=1) as psum:
        offsets = keep.tile([P, S // 16], U16, name="offsets")
        words_all = keep.tile([P, T], I32, name="words_all")
        scales_all = keep.tile([P, T], U8, name="scales_all")
        w_raw = keep.tile([P, PACK, N], F32, name="w_raw")
        side_all = [keep.tile([P, T], F32, name=f"side_all{t}") for t in range(PACK)]
        warm = keep.tile([P, 8], F32, name="warm")
        warm_out = keep.tile([P, 8], F32, name="warm_out")

        nc.vector.memset(scales_all[:].bitcast(I32), 0)
        nc.gpsimd.memset(warm[:], 0.0)
        nc.scalar.activation(warm_out[:], warm[:], SIGMOID)

        side_rows = side.rearrange("(p t) c -> p t c", t=PACK)
        nc.sync.dma_start(words_all[:], x_words[0].rearrange("p c r -> p (c r)").bitcast(I32))
        nc.sync.dma_start(offsets[:], offs)
        for q in range(QUADRANTS):
            nc.sync.dma_start(scales_all[32 * q : 32 * q + 4, :].bitcast(I32), x_scales[0, 4 * q : 4 * q + 4, :].bitcast(I32))
        nc.sync.dma_start(side_all[0][:], side_rows[:, 0, :])
        nc.sync.dma_start(w_raw[:], w1.rearrange("(p j) c -> p j c", j=PACK))
        for t in range(1, PACK):
            nc.sync.dma_start(side_all[t][:], side_rows[:, t, :])

        x_codes = keep.tile([P, S], U32, name="x_codes", align_bytes=64)
        nc.vector.tensor_copy(x_codes[:], words_all[:].bitcast(U32).indirect(offsets[:]))
        x_bytes = keep.tile([P, S], U8, name="x_bytes", align_bytes=64)
        nc.vector.tensor_copy(x_bytes[:], scales_all[:].indirect(offsets[:]))

        gates = [keep.tile([P, S], F32, name=f"gate{t}") for t in range(PACK)]

        def look_up(t, a, b):
            nc.scalar.activation(gates[t][:, a:b], side_all[t][:].indirect(offsets[:, a // 16 : b // 16]), SIGMOID)

        look_up(0, 0, S)

        w_bf = keep.tile([P, PACK, P, PACK], BF16, name="w_bf", align_bytes=64)
        w_dst = w_bf[:].rearrange("p t m j -> p m j t")
        w_src = w_raw[:].rearrange("p j (m t) -> p m j t", t=PACK)
        nc.vector.tensor_copy(w_dst[:, :, :, :2], w_src[:, :, :, :2])
        nc.scalar.copy(w_dst[:, :, :, 2:], w_src[:, :, :, 2:])

        spans = {t: [(0, HALF), (HALF, S)] if t == 0 else [(0, S)] for t in range(PACK)}
        banks = {(t, span): psum.tile([P, span[1] - span[0]], F32, name=f"acc{t}_{span[0]}") for t in range(PACK) for span in spans[t]}

        def product(t, a, b):
            span = [span for span in spans[t] if span[0] <= a and b <= span[1]][0]
            return banks[t, span][:, a - span[0] : b - span[0]]

        for t0, t1 in [(0, 1), (1, 2), (2, 4)]:
            w_codes = keep.tile([P, (t1 - t0) * P], U32, name=f"w_codes{t0}", align_bytes=64)
            w_bytes = keep.tile([P, (t1 - t0) * P], U8, name=f"w_bytes{t0}", align_bytes=64)
            nc.vector.quantize_mx(out=w_codes[:].bitcast(FP8X4), scales=w_bytes[:],
                                  in_=w_bf[:, t0:t1, :, :].rearrange("p t m j -> p (t m j)"))
            for t in range(t0, t1):
                cols = slice((t - t0) * P, (t - t0 + 1) * P)
                for a, b in spans[t]:
                    nc.tensor.matmul_mx(out=product(t, a, b), lhsT=w_codes[:, cols].bitcast(FP8X4), lhsT_scale=w_bytes[:, cols],
                                        rhs=x_codes[:, a:b].bitcast(FP8X4), rhs_scale=x_bytes[:, a:b], start=True, stop=True)

        y = keep.tile([P, PACK, S], F32, name="y")
        out_rows = out_0.rearrange("(p t) s -> p (t s)", t=PACK)
        woven = keep.tile([P, S, PACK], BF16, name="woven", align_bytes=64)
        y_codes = keep.tile([P, S], U32, name="y_codes", align_bytes=64)
        y_bytes = keep.tile([P, S], U8, name="y_bytes", align_bytes=64)
        words_out = out_1[0].rearrange("p c r -> p (c r)").bitcast(I32)

        def multiply(t, a, b):
            nc.vector.tensor_tensor(y[:, t, a:b], product(t, a, b), gates[t][:, a:b], MULT)

        def pair(t, a, b):
            return woven[:, a:b, t : t + 2], y[:, t : t + 2, a:b].rearrange("p t c -> p c t")

        def quantise(a, b):
            nc.vector.quantize_mx(out=y_codes[:, a:b].bitcast(FP8X4), scales=y_bytes[:, a:b],
                                  in_=woven[:, a:b, :].rearrange("p c t -> p (c t)"))

        def store_rows(a, b):
            nc.sync.dma_start(out_rows[:, a:b], y[:].rearrange("p t s -> p (t s)")[:, a:b])

        def store_words(a, b):
            nc.sync.dma_start(words_out[:, a:b], y_codes[:, a:b].bitcast(I32))

        first, second, third, fourth = [(a, a + QUARTER) for a in range(0, S, QUARTER)]

        def weave_gpsimd(t, a, b):
            dst, src = pair(t, a, b)
            nc.gpsimd.tensor_scalar(dst, src, 1.0, -0.0, MULT, ADD)

        picked = keep.tile([P, PICKED], F32, name="picked")
        nc.vector.tensor_copy(picked[:], side_all[1][:].indirect(offsets[:, (S - PICKED) // 16 :]))
        for a, b in spans[0]:
            multiply(0, a, b)
        look_up(1, 0, PICKED)
        look_up(1, PICKED, S - PICKED)
        nc.scalar.activation(gates[1][:, S - PICKED :], picked[:], SIGMOID)
        multiply(1, 0, PICKED)
        multiply(1, PICKED, S - PICKED)
        store_rows(0, 2 * S - PICKED)
        nc.vector.tensor_copy(*pair(0, *first))
        multiply(1, *fourth)
        multiply(1, S - PICKED, third[1])
        nc.vector.tensor_copy(*pair(0, *fourth))
        weave_gpsimd(0, second[0], third[1])
        look_up(2, 0, S)
        multiply(2, 0, S)
        store_rows(2 * S - PICKED, 3 * S)

        for u in (first, second, third, fourth):
            look_up(3, *u)
        multiply(3, *first)
        multiply(3, *second)
        nc.scalar.copy(*pair(2, *second))
        nc.vector.tensor_copy(*pair(2, *first))
        multiply(3, *third)
        nc.scalar.copy(*pair(2, *third))
        multiply(3, *fourth)
        store_rows(3 * S, 4 * S)
        quantise(*first)
        nc.vector.tensor_copy(*pair(2, *fourth))
        quantise(*second)
        store_words(0, HALF)
        quantise(*third)
        quantise(*fourth)
        store_words(HALF, S)

        for q in range(QUADRANTS):
            queue = nc.sync if q == 1 else nc.scalar
            queue.dma_start(out_2[0, 4 * q : 4 * q + 4, :].bitcast(I32), y_bytes[32 * q : 32 * q + 4, :].bitcast(I32))
